import numpy as np
import ml_dtypes


def mxq(x, axis, fmt="e4m3"):
    dtype, down = {"e4m3": (ml_dtypes.float8_e4m3fn, 7), "e5m2": (ml_dtypes.float8_e5m2, 14)}[fmt]
    v = np.moveaxis(np.asarray(x, np.float32).astype(ml_dtypes.bfloat16).astype(np.float64), axis, -1)
    blocks = v.reshape(v.shape[:-1] + (-1, 32))
    amax = np.abs(blocks).max(-1, keepdims=True)
    byte = np.maximum(np.where(amax > 0, np.frexp(amax)[1] - 1 + 127, 0) - down, 1)
    scale = np.exp2(byte - 127.0)
    codes = (blocks / scale).astype(np.float32).astype(dtype).astype(np.float64)
    return np.moveaxis((codes * scale).reshape(v.shape), -1, axis)


WIDE = False


def mx_kscale(k):
    if not WIDE:
        return np.ones(k)
    levels = np.array([10, -10, 5, -5, 0])
    if k % 512:
        return np.exp2(np.random.permutation(np.resize(levels, k // 32))).repeat(32)
    a = np.empty((k // 512, 16))
    for p in range(k // 512):
        a[p, :8] = np.random.permutation(np.resize(levels, 8))
        for g in range(8):
            far = levels[np.abs(levels - a[p, g]) >= 10]
            a[p, g + 8] = far[np.random.randint(len(far))]
    return np.exp2(a.ravel()).repeat(32)


BF16 = ml_dtypes.bfloat16


def bf(x):
    return np.asarray(x, np.float32).astype(BF16)


def f64(x):
    return np.asarray(x).astype(np.float64)


E2M1 = np.array([0.0, 0.5, 1.0, 1.5, 2.0, 3.0, 4.0, 6.0, -0.0, -0.5, -1.0, -1.5, -2.0, -3.0, -4.0, -6.0])


def pack_weight(w, fmt):
    k, n = w.shape
    w = f64(bf(w)).reshape(k // 32, 32, n)
    amax = np.abs(w).max(1)
    if fmt == "e4m3":
        byte = np.frexp(amax)[1] - 1 + 127 - 7
    else:
        mant, ex = np.frexp(amax / 6.0)
        byte = np.where(mant > 0.5, ex, ex - 1) + 127
    byte = np.clip(np.where(amax > 0, byte, 1), 1, 254)
    scaled = (w * np.exp2(127.0 - byte)[:, None, :]).reshape(k, n).astype(np.float32)
    by_word = np.ascontiguousarray(scaled.reshape(k // 512, 128, 4, n).transpose(0, 1, 3, 2))
    if fmt == "e4m3":
        words = by_word.astype(ml_dtypes.float8_e4m3fn).view(np.uint8)
    else:
        c = by_word.astype(ml_dtypes.float4_e2m1fn).view(np.uint8) & 0xF
        words = c[..., 0::2] | (c[..., 1::2] << 4)
    return np.ascontiguousarray(words), np.ascontiguousarray(byte.astype(np.uint8).reshape(k // 512, 16, n))


def unpack_weight(words, scales, fmt):
    g, p, n, _ = words.shape
    if fmt == "e4m3":
        vals = np.ascontiguousarray(words).view(ml_dtypes.float8_e4m3fn).astype(np.float64)
    else:
        nib = np.empty((g, p, n, 4), np.uint8)
        nib[..., 0::2] = words & 0xF
        nib[..., 1::2] = words >> 4
        vals = E2M1[nib]
    vals = vals * np.repeat(np.exp2(scales.astype(np.float64) - 127.0), 8, axis=1)[..., None]
    return vals.transpose(0, 1, 3, 2).reshape(g * 512, n)
def pack4(w):
    words, scales = pack_weight(w, "e2m1")
    return words.reshape(words.shape[0], 128, -1), scales


def unpack4(words, scales):
    return unpack_weight(words.reshape(words.shape[0], 128, -1, 2), scales, "e2m1")


M, D, F, R, N = 512, 1024, 2048, 512, 1536


def setup_inputs():
    s = mx_kscale(D)
    r = mx_kscale(R)
    t = mx_kscale(F)
    x = np.random.standard_normal((M, D)) * s
    w_up = np.random.standard_normal((D, F)) / np.sqrt(D) / s[:, None] * t
    score_a = np.random.standard_normal((F, R)) * r
    score_b = 2.0 * np.random.standard_normal((R, N)) / np.sqrt(R) / r[:, None]
    w_down = 2.0 * np.random.standard_normal((F, N)) / np.sqrt(F) / t[:, None]
    w_up_words, w_up_scales = pack4(w_up)
    return {"x": bf(x), "w_up_words": w_up_words, "w_up_scales": w_up_scales,
            "score_a": bf(score_a), "score_b": bf(score_b), "w_down": bf(w_down)}


def reference(x, w_up_words, w_up_scales, score_a, score_b, w_down):
    w_up = unpack4(w_up_words, w_up_scales)
    h = np.maximum(mxq(f64(x), 1, "e4m3") @ w_up, 0.0)
    z = mxq(f64(score_a), 1, "e4m3") @ mxq(f64(score_b), 0, "e4m3")
    mask = 1.0 / (1.0 + np.exp(-z))
    w_masked = f64(w_down) * mask
    return mxq(h, 1, "e4m3") @ mxq(w_masked, 0, "e4m3")

@@ -1,0 +1,364 @@
+from contextlib import ExitStack
+
+import concourse.mybir as mybir
+from concourse.masks import make_identity
+
+M, D, F, R, N = 512, 1024, 2048, 512, 1536
+FLOPS = 2 * (M * D * F + F * R * N + M * F * N)
+
+F32 = mybir.dt.float32
+BF16 = mybir.dt.bfloat16
+I32 = mybir.dt.int32
+U32 = mybir.dt.uint32
+U8 = mybir.dt.uint8
+FP8X4 = mybir.dt.float8_e4m3fn_x4
+FP4X4 = mybir.dt.float4_e2m1fn_x4
+ACT = mybir.ActivationFunctionType
+
+P = 128
+PACK = 4
+K_PASS = P * PACK
+BANK = 512
+D_PASSES = D // K_PASS
+F_PASSES = F // K_PASS
+TOKEN_TILES = M // P
+WIDTHS = (512, 512, 256, 256)
+STARTS = tuple(sum(WIDTHS[:c]) for c in range(len(WIDTHS)))
+B_LOADS = N // BANK
+RUN = 2
+
+
+def tile_sigmoid_masked_down_projection_s11_kernel(
+    tc, x, w_up_words, w_up_scales, score_a, score_b, w_down, out
+):
+    nc = tc.nc
+    with ExitStack() as ctx:
+        sb = ctx.enter_context(tc.tile_pool(name="sb", bufs=1))
+        psum = ctx.enter_context(tc.psum_pool(name="psum", bufs=1))
+        ctx.enter_context(tc.manual_schedule())
+
+        raw = {}
+        codes = {}
+        scales = {}
+        grouped = {}
+        banks = {}
+        mask = {}
+        turn = {"z": 0, "other": 0}
+
+        def take_bank(role, key):
+            index = turn[role] % 4 + (0 if role == "z" else 4)
+            turn[role] = turn[role] + 1
+            bank = psum.tile([P, BANK], F32, name="bank%d" % index, tag="bank%d" % index)
+            banks[key] = bank
+            return bank
+
+        def copy_on(engine, out_ap, in_ap):
+            if engine == "scalar":
+                nc.scalar.copy(out=out_ap, in_=in_ap)
+            else:
+                nc.vector.tensor_copy(out=out_ap, in_=in_ap)
+
+        def new_planes(key, tag, width, bufs):
+            codes[key] = sb.tile([P, width], U32, name=tag + "_codes", tag=tag + "_codes", bufs=bufs, align_bytes=64)
+            scales[key] = sb.tile([P, width], U8, name=tag + "_scales", tag=tag + "_scales", bufs=bufs, align_bytes=64)
+
+        def quantize_part(key, cols, source):
+            nc.vector.quantize_mx(out=codes[key][:, cols].bitcast(FP8X4), scales=scales[key][:, cols], in_=source)
+
+        def quantize(key, tag, bufs):
+            width = grouped[key].shape[1] // PACK
+            new_planes(key, tag, width, bufs)
+            quantize_part(key, slice(0, width), grouped[key][:])
+
+        def load_f_rows(key, source, g, cols, tag, bufs):
+            width = cols.stop - cols.start
+            raw[key] = sb.tile([P, PACK, width], BF16, name=tag, tag=tag, bufs=bufs)
+            rows = source[g * K_PASS : (g + 1) * K_PASS, cols].rearrange("(j t e) n -> e j t n", t=PACK, e=4)
+            for e in range(4):
+                nc.sync.dma_start(out=raw[key][e:P:4, :, :], in_=rows[e])
+
+        def load_score_a(g):
+            load_f_rows(("a", g), score_a, g, slice(0, R), "a_raw", F_PASSES)
+
+        def load_w(b, g):
+            load_f_rows(("w", b, g), w_down, g, slice(b * BANK, (b + 1) * BANK), "w_raw", B_LOADS * F_PASSES)
+
+        def load_score_b(b, half):
+            raw["b", b, half] = sb.tile([P, PACK, 256], BF16, name="b_raw", tag="b_raw", bufs=2 * B_LOADS)
+            cols = score_b[:, b * BANK + half * 256 : b * BANK + (half + 1) * 256]
+            nc.sync.dma_start(out=raw["b", b, half][:], in_=cols.rearrange("(p t) n -> p t n", t=PACK))
+
+        def load_x(m):
+            raw["x", m] = sb.tile([P, D], BF16, name="x_raw", tag="x_raw", bufs=TOKEN_TILES)
+            nc.sync.dma_start(out=raw["x", m][:], in_=x[m * P : (m + 1) * P, :])
+
+        def load_up_codes(g):
+            raw["up", g] = sb.tile([P, D_PASSES, 256], I32, name="up_raw", tag="up_raw", bufs=F_PASSES)
+            words = w_up_words.bitcast(I32)[:, :, g * 256 : (g + 1) * 256]
+            nc.sync.dma_start(out=raw["up", g][:], in_=words.rearrange("a p w -> p a w"))
+
+        def load_up_scales():
+            rows = w_up_scales.bitcast(I32)
+            for q in range(4):
+                nc.sync.dma_start(
+                    out=up_scale_raw[32 * q : 32 * q + 4, :, :],
+                    in_=rows[:, 4 * q : 4 * q + 4, :].rearrange("a r w -> r a w"),
+                )
+
+        def sort_up(g):
+            codes["up", g] = sb.tile([P, D_PASSES * 1024], U8, name="up_codes", tag="up_codes", bufs=F_PASSES, align_bytes=64)
+            scales["up", g] = sb.tile([P, D_PASSES * 512], U8, name="up_scales", tag="up_scales", bufs=F_PASSES, align_bytes=64)
+            nc.vector.tensor_copy(
+                out=codes["up", g][:].bitcast(I32).rearrange("p (a t j w) -> p a t j w", a=D_PASSES, t=PACK, w=2),
+                in_=raw["up", g][:].rearrange("p a (j t w) -> p a t j w", t=PACK, w=2),
+            )
+            nc.vector.tensor_copy(
+                out=scales["up", g][:].bitcast(I32).rearrange("p (a t j) -> p a t j", a=D_PASSES, t=PACK),
+                in_=up_scale_raw[:, :, g * P : (g + 1) * P].rearrange("p a (j t) -> p a t j", t=PACK),
+            )
+
+        def transpose_pair(key, words):
+            bank = take_bank("other", key)
+            for s in range(2):
+                for u in range(2):
+                    column = (2 * s + u) * P
+                    nc.tensor.transpose(
+                        bank[:, column : column + P], words[:, 256 * s + u : 256 * (s + 1) : 2], identity[:]
+                    )
+
+        def transpose_a(g):
+            words = raw["a", g][:].rearrange("p t k -> p (t k)").bitcast(F32)
+            for half in range(2):
+                transpose_pair(("a", g, half), words[:, half * BANK : (half + 1) * BANK])
+
+        def transpose_x(m):
+            transpose_pair(("x", m), raw["x", m][:].bitcast(F32))
+
+        def gather_words(engine, target, bank):
+            copy_on(
+                engine,
+                target.rearrange("p (s r u) -> p s r u", s=2, u=2),
+                bank[:].rearrange("p (s u r) -> p s r u", s=2, u=2),
+            )
+
+        def empty_a(g, half, engine):
+            if half == 0:
+                grouped["a", g] = sb.tile([P, PACK * K_PASS], BF16, name="a_grouped", tag="a_grouped", bufs=2, align_bytes=64)
+            words = grouped["a", g][:].bitcast(F32)
+            gather_words(engine, words[:, half * BANK : (half + 1) * BANK], banks["a", g, half])
+
+        def empty_x(m, engine):
+            grouped["x", m] = sb.tile([P, D], BF16, name="x_grouped", tag="x_grouped", bufs=2, align_bytes=64)
+            gather_words(engine, grouped["x", m][:].bitcast(F32), banks["x", m])
+
+        def interleave_b(b, half):
+            grouped["b", b, half] = sb.tile([P, PACK * 256], BF16, name="b_grouped", tag="b_grouped", bufs=2, align_bytes=64)
+            nc.vector.tensor_copy(
+                out=grouped["b", b, half][:].rearrange("p (c i t) -> p c t i", i=4, t=PACK),
+                in_=raw["b", b, half][:].rearrange("p t (c i) -> p c t i", i=4),
+            )
+
+        def quantize_b(b, half):
+            if half == 0:
+                new_planes(("b", b), "b", BANK, B_LOADS)
+            quantize_part(("b", b), slice(half * 256, (half + 1) * 256), grouped["b", b, half][:])
+
+        def quantize_a_half(g, half):
+            if half == 0:
+                new_planes(("a", g), "a", K_PASS, F_PASSES)
+            quantize_part(("a", g), slice(half * 256, (half + 1) * 256), grouped["a", g][:, half * 1024 : (half + 1) * 1024])
+
+        def mx(out_ap, stationary, s_cols, moving, m_cols, start, stop):
+            nc.tensor.matmul_mx(
+                out=out_ap,
+                lhsT=codes[stationary][:, s_cols].bitcast(FP8X4),
+                lhsT_scale=scales[stationary][:, s_cols],
+                rhs=codes[moving][:, m_cols].bitcast(FP8X4),
+                rhs_scale=scales[moving][:, m_cols],
+                start=start,
+                stop=stop,
+            )
+
+        def matmul_h(g, m):
+            bank = take_bank("other", ("h", g, m))
+            for t in range(PACK):
+                for a in range(D_PASSES):
+                    column = (a * PACK + t) * P
+                    nc.tensor.matmul_mx(
+                        out=bank[:, t * P : (t + 1) * P],
+                        lhsT=codes["up", g][:, 2 * column : 2 * (column + P)].bitcast(FP4X4),
+                        lhsT_scale=scales["up", g][:, column : column + P],
+                        rhs=codes["x", m][:, a * P : (a + 1) * P].bitcast(FP8X4),
+                        rhs_scale=scales["x", m][:, a * P : (a + 1) * P],
+                        start=(a == 0),
+                        stop=(a == D_PASSES - 1),
+                    )
+
+        def relu_h(g, m, engine):
+            if m == 0:
+                grouped["h", g] = sb.tile([P, PACK * M], BF16, name="h_grouped", tag="h_grouped", bufs=2, align_bytes=64)
+            target = grouped["h", g][:, m * BANK : (m + 1) * BANK].rearrange("p (r t) -> p r t", t=PACK)
+            sums = banks["h", g, m][:].rearrange("p (t r) -> p r t", t=PACK)
+            if engine == "scalar":
+                nc.scalar.activation(out=target, in_=sums, func=ACT.Relu)
+            else:
+                nc.vector.tensor_scalar_max(target, sums, 0.0)
+
+        def matmul_z(c, g):
+            width = WIDTHS[c]
+            per_bank = BANK // width
+            b, first = divmod(STARTS[c], BANK)
+            for t in range(PACK):
+                if t % per_bank == 0:
+                    bank = take_bank("z", ("z", c, g, t // per_bank))
+                column = (t % per_bank) * width
+                mx(bank[:, column : column + width], ("a", g), slice(t * P, (t + 1) * P), ("b", b), slice(first, first + width), True, True)
+
+        def sigmoid_z(c, g):
+            mask[c, g] = sb.tile([P, PACK * WIDTHS[c]], F32, name="mask", tag="mask", bufs=3)
+            for s in range(PACK * WIDTHS[c] // BANK):
+                nc.scalar.activation(out=mask[c, g][:, s * BANK : (s + 1) * BANK], in_=banks["z", c, g, s][:], func=ACT.Sigmoid)
+
+        def multiply(c, g):
+            width = WIDTHS[c]
+            grouped["w", c, g] = sb.tile([P, PACK * width], BF16, name="w_grouped", tag="w_grouped", bufs=3, align_bytes=64)
+            b, first = divmod(STARTS[c], BANK)
+            weights = raw["w", b, g][:, :, first : first + width]
+            nc.vector.tensor_tensor(
+                out=grouped["w", c, g][:].rearrange("p (c i t) -> p c t i", i=RUN, t=PACK),
+                in0=mask[c, g][:].rearrange("p (t c i) -> p c t i", t=PACK, i=RUN),
+                in1=weights.rearrange("p t (c i) -> p c t i", i=RUN),
+                op=mybir.AluOpType.mult,
+            )
+
+        def quantize_w(c, g):
+            quantize(("w", c, g), "w%d" % WIDTHS[c], 8 if WIDTHS[c] == BANK else 6)
+
+        def matmul_out(c, m, passes):
+            width = WIDTHS[c]
+            if passes[0] == 0:
+                take_bank("other", ("out", c, m))
+            for g in passes:
+                mx(banks["out", c, m][:, 0:width], ("h", g), slice(m * P, (m + 1) * P), ("w", c, g), slice(0, width), g == 0, g == F_PASSES - 1)
+
+        def store_out(c, m, engine):
+            width = WIDTHS[c]
+            result = sb.tile([P, width], F32, name="result", tag="result", bufs=4)
+            copy_on(engine, result[:], banks["out", c, m][:, 0:width])
+            nc.sync.dma_start(out=out[m * P : (m + 1) * P, STARTS[c] : STARTS[c] + width], in_=result[:])
+
+        identity = sb.tile([P, P], F32, name="identity")
+        make_identity(nc, identity[:])
+        up_scale_raw = sb.tile([P, D_PASSES, F // 4], I32, name="up_scale_raw")
+        nc.gpsimd.memset(up_scale_raw[:], 0)
+
+        tokens = range(TOKEN_TILES)
+        all_passes = list(range(F_PASSES))
+        load_score_a(0)
+        load_score_b(0, 0)
+        load_score_b(0, 1)
+        load_x(0)
+        load_x(1)
+        load_score_b(1, 0)
+        load_score_b(1, 1)
+        load_x(2)
+        load_x(3)
+        load_w(0, 0)
+        load_up_scales()
+        load_up_codes(0)
+        load_score_a(1)
+        load_w(1, 0)
+        for g in range(1, F_PASSES):
+            load_up_codes(g)
+            if g + 1 < F_PASSES:
+                load_score_a(g + 1)
+            load_w(0, g)
+        for g in range(1, F_PASSES):
+            load_w(1, g)
+        load_score_b(2, 0)
+        load_score_b(2, 1)
+        for g in range(F_PASSES):
+            load_w(2, g)
+
+        transpose_a(0)
+        interleave_b(0, 0)
+        empty_a(0, 0, "scalar")
+        interleave_b(0, 1)
+        quantize_b(0, 0)
+        empty_a(0, 1, "scalar")
+        quantize_a_half(0, 0)
+        quantize_b(0, 1)
+        quantize_a_half(0, 1)
+        transpose_x(0)
+        empty_x(0, "scalar")
+        transpose_x(1)
+        empty_x(1, "scalar")
+        matmul_z(0, 0)
+        sigmoid_z(0, 0)
+        interleave_b(1, 0)
+        interleave_b(1, 1)
+        quantize_b(1, 0)
+        quantize_b(1, 1)
+        quantize(("x", 0), "x", TOKEN_TILES)
+        quantize(("x", 1), "x", TOKEN_TILES)
+        matmul_z(1, 0)
+        sigmoid_z(1, 0)
+        transpose_x(2)
+        transpose_x(3)
+        multiply(0, 0)
+        sort_up(0)
+        empty_x(2, "vector")
+        empty_x(3, "vector")
+        quantize(("x", 2), "x", TOKEN_TILES)
+        quantize(("x", 3), "x", TOKEN_TILES)
+        units = [(0, 0), (1, 0), (0, 1), (0, 2), (0, 3), (1, 1), (1, 2), (1, 3)] + [(c, g) for c in (2, 3) for g in range(F_PASSES)]
+        transpose_a(1)
+        empty_a(1, 0, "scalar")
+        empty_a(1, 1, "scalar")
+        quantize(("a", 1), "a", F_PASSES)
+        multiply(1, 0)
+        quantize_w(0, 0)
+        for u in range(2, len(units)):
+            c, g = units[u]
+            hg = u - 2
+            if hg < F_PASSES:
+                matmul_h(hg, 0)
+                relu_h(hg, 0, "scalar")
+                matmul_h(hg, 1)
+                relu_h(hg, 1, "scalar")
+            if u < 4:
+                transpose_a(u)
+                empty_a(u, 0, "scalar")
+                empty_a(u, 1, "scalar")
+            matmul_z(c, g)
+            sigmoid_z(c, g)
+            if hg < F_PASSES:
+                matmul_h(hg, 2)
+                relu_h(hg, 2, "scalar")
+                matmul_h(hg, 3)
+                relu_h(hg, 3, "scalar")
+            outs = {7: [(0, 0), (0, 1)], 8: [(0, 2)], 9: [(0, 3)], 10: [(1, 0)], 11: [(1, 1)], 12: [(1, 2)], 13: [(1, 3)], 14: [(2, 0), (2, 1)], 15: [(2, 2), (2, 3)]}.get(u, [])
+            for oc, m in outs:
+                matmul_out(oc, m, all_passes)
+                store_out(oc, m, "scalar")
+            if u < 4:
+                quantize(("a", u), "a", F_PASSES)
+            if hg + 1 < F_PASSES:
+                sort_up(hg + 1)
+            if u == 5:
+                interleave_b(2, 0)
+                interleave_b(2, 1)
+                quantize_b(2, 0)
+                quantize_b(2, 1)
+            multiply(c, g)
+            quantize_w(*units[u - 1])
+            if hg < F_PASSES:
+                quantize(("h", hg), "h", F_PASSES)
+        last = len(WIDTHS) - 1
+        for g in range(F_PASSES - 1):
+            for m in tokens:
+                matmul_out(last, m, [g])
+        quantize_w(*units[-1])
+        for m in tokens:
+            matmul_out(last, m, all_passes[3:])
+            store_out(last, m, "scalar" if m % 2 == 0 else "vector")

@@ -25,7 +25,7 @@ TOKEN_TILES = M // P
 WIDTHS = (512, 512, 256, 256)
 STARTS = tuple(sum(WIDTHS[:c]) for c in range(len(WIDTHS)))
 B_LOADS = N // BANK
-RUN = 2
+RUN = 4
 
 
 def tile_sigmoid_masked_down_projection_s11_kernel(
@@ -80,13 +80,22 @@ def tile_sigmoid_masked_down_projection_s11_kernel(
         def load_score_a(g):
             load_f_rows(("a", g), score_a, g, slice(0, R), "a_raw", F_PASSES)
 
-        def load_w(b, g):
-            load_f_rows(("w", b, g), w_down, g, slice(b * BANK, (b + 1) * BANK), "w_raw", B_LOADS * F_PASSES)
+        def load_score_a_half(g, half):
+            raw["a", g, half] = sb.tile([P, 2, R], BF16, name="a_first", tag="a_first", bufs=2)
+            rows = score_a[g * K_PASS : (g + 1) * K_PASS, :].rearrange("(j t e) n -> e j t n", t=PACK, e=4)
+            for e in range(4):
+                nc.sync.dma_start(out=raw["a", g, half][e:P:4, :, :], in_=rows[e][:, 2 * half : 2 * half + 2, :])
 
-        def load_score_b(b, half):
-            raw["b", b, half] = sb.tile([P, PACK, 256], BF16, name="b_raw", tag="b_raw", bufs=2 * B_LOADS)
-            cols = score_b[:, b * BANK + half * 256 : b * BANK + (half + 1) * 256]
-            nc.sync.dma_start(out=raw["b", b, half][:], in_=cols.rearrange("(p t) n -> p t n", t=PACK))
+        def transpose_a_half(g, half):
+            transpose_pair(("a", g, half), raw["a", g, half][:].rearrange("p t k -> p (t k)").bitcast(F32))
+
+        def load_w(b, g):
+            load_f_rows(("w", b, g), w_down, g, slice(b * BANK, (b + 1) * BANK), "w_raw", 10)
+
+        def load_score_b(b):
+            raw["b", b] = sb.tile([P, PACK, BANK], BF16, name="b_raw", tag="b_raw", bufs=B_LOADS)
+            cols = score_b[:, b * BANK : (b + 1) * BANK]
+            nc.sync.dma_start(out=raw["b", b][:], in_=cols.rearrange("(p t) n -> p t n", t=PACK))
 
         def load_x(m):
             raw["x", m] = sb.tile([P, D], BF16, name="x_raw", tag="x_raw", bufs=TOKEN_TILES)
@@ -97,13 +106,17 @@ def tile_sigmoid_masked_down_projection_s11_kernel(
             words = w_up_words.bitcast(I32)[:, :, g * 256 : (g + 1) * 256]
             nc.sync.dma_start(out=raw["up", g][:], in_=words.rearrange("a p w -> p a w"))
 
-        def load_up_scales():
-            rows = w_up_scales.bitcast(I32)
+        def load_up_scales(first, count):
+            plane = sb.tile([P, D_PASSES, count * P], I32, name="up_scale_raw%d" % first)
+            nc.gpsimd.memset(plane[:], 0)
+            rows = w_up_scales.bitcast(I32)[:, :, first * P : (first + count) * P]
             for q in range(4):
                 nc.sync.dma_start(
-                    out=up_scale_raw[32 * q : 32 * q + 4, :, :],
+                    out=plane[32 * q : 32 * q + 4, :, :],
                     in_=rows[:, 4 * q : 4 * q + 4, :].rearrange("a r w -> r a w"),
                 )
+            for g in range(count):
+                raw["up_scales", first + g] = plane[:, :, g * P : (g + 1) * P]
 
         def sort_up(g):
             codes["up", g] = sb.tile([P, D_PASSES * 1024], U8, name="up_codes", tag="up_codes", bufs=F_PASSES, align_bytes=64)
@@ -114,7 +127,7 @@ def tile_sigmoid_masked_down_projection_s11_kernel(
             )
             nc.vector.tensor_copy(
                 out=scales["up", g][:].bitcast(I32).rearrange("p (a t j) -> p a t j", a=D_PASSES, t=PACK),
-                in_=up_scale_raw[:, :, g * P : (g + 1) * P].rearrange("p a (j t) -> p a t j", t=PACK),
+                in_=raw["up_scales", g].rearrange("p a (j t) -> p a t j", t=PACK),
             )
 
         def transpose_pair(key, words):
@@ -155,7 +168,7 @@ def tile_sigmoid_masked_down_projection_s11_kernel(
             grouped["b", b, half] = sb.tile([P, PACK * 256], BF16, name="b_grouped", tag="b_grouped", bufs=2, align_bytes=64)
             nc.vector.tensor_copy(
                 out=grouped["b", b, half][:].rearrange("p (c i t) -> p c t i", i=4, t=PACK),
-                in_=raw["b", b, half][:].rearrange("p t (c i) -> p c t i", i=4),
+                in_=raw["b", b][:, :, half * 256 : (half + 1) * 256].rearrange("p t (c i) -> p c t i", i=4),
             )
 
         def quantize_b(b, half):
@@ -232,133 +245,224 @@ def tile_sigmoid_masked_down_projection_s11_kernel(
             )
 
         def quantize_w(c, g):
-            quantize(("w", c, g), "w%d" % WIDTHS[c], 8 if WIDTHS[c] == BANK else 6)
+            quantize(("w", c, g), "w%d" % WIDTHS[c], 8 if WIDTHS[c] == BANK else 5)
 
         def matmul_out(c, m, passes):
             width = WIDTHS[c]
+            shared = c == 2 and m >= 2
             if passes[0] == 0:
-                take_bank("other", ("out", c, m))
+                if shared:
+                    banks["out", c, m] = banks["out", c, m - 2]
+                else:
+                    take_bank("z" if c == 3 else "other", ("out", c, m))
+            first = width if shared else 0
             for g in passes:
-                mx(banks["out", c, m][:, 0:width], ("h", g), slice(m * P, (m + 1) * P), ("w", c, g), slice(0, width), g == 0, g == F_PASSES - 1)
+                mx(banks["out", c, m][:, first : first + width], ("h", g), slice(m * P, (m + 1) * P), ("w", c, g), slice(0, width), g == 0, g == F_PASSES - 1)
 
         def store_out(c, m, engine):
             width = WIDTHS[c]
-            result = sb.tile([P, width], F32, name="result", tag="result", bufs=4)
+            result = sb.tile([P, width], F32, name="result", tag="result", bufs=8)
             copy_on(engine, result[:], banks["out", c, m][:, 0:width])
             nc.sync.dma_start(out=out[m * P : (m + 1) * P, STARTS[c] : STARTS[c] + width], in_=result[:])
 
+        def store_pair(c, m, engine):
+            width = WIDTHS[c]
+            result = sb.tile([P, 2 * width], F32, name="result", tag="result", bufs=8)
+            copy_on(engine, result[:], banks["out", c, m][:])
+            rows = out[:, STARTS[c] : STARTS[c] + width].rearrange("(h m p) n -> m p h n", h=2, p=P)
+            nc.sync.dma_start(out=rows[m], in_=result[:].rearrange("p (h n) -> p h n", h=2))
+
+        def hidden(g, m, engine="scalar"):
+            matmul_h(g, m)
+            relu_h(g, m, engine)
+
+        def turn_a(g, first_engine, second_engine):
+            transpose_a(g)
+            empty_a(g, 0, first_engine)
+            empty_a(g, 1, second_engine)
+
+        def gate(c, g):
+            matmul_z(c, g)
+            sigmoid_z(c, g)
+
+        def prepare_b(b):
+            interleave_b(b, 0)
+            interleave_b(b, 1)
+            quantize_b(b, 0)
+            quantize_b(b, 1)
+
+        def quantize_x(m):
+            quantize(("x", m), "x", TOKEN_TILES)
+
+        def quantize_a(g):
+            quantize(("a", g), "a", F_PASSES)
+
+        def quantize_h(g):
+            quantize(("h", g), "h", F_PASSES)
+
+        def out_pass(c, g):
+            for m in range(TOKEN_TILES):
+                matmul_out(c, m, [g])
+
+        def store_chunk(c):
+            for m in range(TOKEN_TILES):
+                store_out(c, m, "scalar")
+
         identity = sb.tile([P, P], F32, name="identity")
         make_identity(nc, identity[:])
-        up_scale_raw = sb.tile([P, D_PASSES, F // 4], I32, name="up_scale_raw")
-        nc.gpsimd.memset(up_scale_raw[:], 0)
 
         tokens = range(TOKEN_TILES)
-        all_passes = list(range(F_PASSES))
         load_score_a(0)
-        load_score_b(0, 0)
-        load_score_b(0, 1)
+        load_score_b(0)
         load_x(0)
         load_x(1)
-        load_score_b(1, 0)
-        load_score_b(1, 1)
+        load_score_b(1)
+        load_up_scales(0, 1)
+        load_up_codes(0)
+        load_w(0, 0)
+        load_score_a(1)
         load_x(2)
         load_x(3)
-        load_w(0, 0)
-        load_up_scales()
-        load_up_codes(0)
-        load_score_a(1)
+        load_up_scales(1, 1)
+        load_up_codes(1)
         load_w(1, 0)
-        for g in range(1, F_PASSES):
-            load_up_codes(g)
-            if g + 1 < F_PASSES:
-                load_score_a(g + 1)
-            load_w(0, g)
-        for g in range(1, F_PASSES):
-            load_w(1, g)
-        load_score_b(2, 0)
-        load_score_b(2, 1)
-        for g in range(F_PASSES):
-            load_w(2, g)
+        load_score_a(2)
+        load_w(0, 1)
+        load_score_a(3)
+        load_up_scales(2, 2)
+        load_up_codes(2)
+        load_w(0, 2)
+        load_score_b(2)
+        load_up_codes(3)
+        load_w(0, 3)
+        load_w(1, 1)
+        load_w(1, 2)
+        load_w(1, 3)
+        load_w(2, 0)
+        load_w(2, 1)
 
-        transpose_a(0)
+        turn_a(0, "scalar", "scalar")
         interleave_b(0, 0)
-        empty_a(0, 0, "scalar")
+        quantize_a_half(0, 0)
         interleave_b(0, 1)
         quantize_b(0, 0)
-        empty_a(0, 1, "scalar")
-        quantize_a_half(0, 0)
         quantize_b(0, 1)
         quantize_a_half(0, 1)
         transpose_x(0)
         empty_x(0, "scalar")
         transpose_x(1)
         empty_x(1, "scalar")
-        matmul_z(0, 0)
-        sigmoid_z(0, 0)
-        interleave_b(1, 0)
-        interleave_b(1, 1)
-        quantize_b(1, 0)
-        quantize_b(1, 1)
-        quantize(("x", 0), "x", TOKEN_TILES)
-        quantize(("x", 1), "x", TOKEN_TILES)
-        matmul_z(1, 0)
-        sigmoid_z(1, 0)
-        transpose_x(2)
-        transpose_x(3)
-        multiply(0, 0)
+        gate(0, 0)
+        quantize_x(0)
+        prepare_b(1)
+        gate(1, 0)
+        quantize_x(1)
         sort_up(0)
-        empty_x(2, "vector")
-        empty_x(3, "vector")
-        quantize(("x", 2), "x", TOKEN_TILES)
-        quantize(("x", 3), "x", TOKEN_TILES)
-        units = [(0, 0), (1, 0), (0, 1), (0, 2), (0, 3), (1, 1), (1, 2), (1, 3)] + [(c, g) for c in (2, 3) for g in range(F_PASSES)]
-        transpose_a(1)
-        empty_a(1, 0, "scalar")
-        empty_a(1, 1, "scalar")
-        quantize(("a", 1), "a", F_PASSES)
-        multiply(1, 0)
+        multiply(0, 0)
+        hidden(0, 0)
+        turn_a(1, "vector", "scalar")
+        hidden(0, 1)
+        transpose_x(2)
+        empty_x(2, "scalar")
+        transpose_x(3)
+        empty_x(3, "scalar")
         quantize_w(0, 0)
-        for u in range(2, len(units)):
+        quantize_a(1)
+        sort_up(1)
+        quantize_x(2)
+        quantize_x(3)
+        multiply(1, 0)
+        load_w(2, 2)
+        load_w(2, 3)
+        units = [(0, 0), (1, 0), (0, 1), (0, 2), (0, 3), (1, 1), (1, 2), (1, 3)] + [(c, g) for c in (2, 3) for g in range(F_PASSES)]
+        for u in range(2, 8):
             c, g = units[u]
             hg = u - 2
-            if hg < F_PASSES:
-                matmul_h(hg, 0)
-                relu_h(hg, 0, "scalar")
-                matmul_h(hg, 1)
-                relu_h(hg, 1, "scalar")
-            if u < 4:
-                transpose_a(u)
-                empty_a(u, 0, "scalar")
-                empty_a(u, 1, "scalar")
-            matmul_z(c, g)
-            sigmoid_z(c, g)
-            if hg < F_PASSES:
-                matmul_h(hg, 2)
-                relu_h(hg, 2, "scalar")
-                matmul_h(hg, 3)
-                relu_h(hg, 3, "scalar")
-            outs = {7: [(0, 0), (0, 1)], 8: [(0, 2)], 9: [(0, 3)], 10: [(1, 0)], 11: [(1, 1)], 12: [(1, 2)], 13: [(1, 3)], 14: [(2, 0), (2, 1)], 15: [(2, 2), (2, 3)]}.get(u, [])
-            for oc, m in outs:
-                matmul_out(oc, m, all_passes)
-                store_out(oc, m, "scalar")
-            if u < 4:
-                quantize(("a", u), "a", F_PASSES)
-            if hg + 1 < F_PASSES:
+            if u == 3:
+                turn_a(u, "scalar", "scalar")
+            gate(c, g)
+            if u == 2:
+                turn_a(u, "scalar", "scalar")
+            if 0 < hg and hg + 1 < F_PASSES:
                 sort_up(hg + 1)
-            if u == 5:
+            if u < 4:
+                quantize_a(u)
+            if 0 < hg <= F_PASSES:
+                quantize_h(hg - 1)
+            if hg < F_PASSES:
+                hidden(hg, 2)
+                hidden(hg, 3)
+            if hg + 1 < F_PASSES:
+                hidden(hg + 1, 0)
+                hidden(hg + 1, 1)
+            if u == 6:
+                out_pass(0, 0)
+                out_pass(0, 1)
+            if u == 7:
+                out_pass(0, 2)
+            if u == 4:
                 interleave_b(2, 0)
+            if u == 5:
                 interleave_b(2, 1)
                 quantize_b(2, 0)
                 quantize_b(2, 1)
+            if u <= 6:
+                quantize_w(*units[u - 1])
             multiply(c, g)
-            quantize_w(*units[u - 1])
-            if hg < F_PASSES:
-                quantize(("h", hg), "h", F_PASSES)
-        last = len(WIDTHS) - 1
-        for g in range(F_PASSES - 1):
-            for m in tokens:
-                matmul_out(last, m, [g])
-        quantize_w(*units[-1])
+        quantize_w(1, 2)
+
+        def mask_and_weigh(c, g):
+            sigmoid_z(c, g)
+            multiply(c, g)
+
+        matmul_z(2, 0)
+        out_pass(0, 3)
+        matmul_z(2, 1)
+        mask_and_weigh(2, 0)
+        quantize_w(1, 3)
+        store_out(0, 0, "scalar")
+        store_out(0, 1, "scalar")
+        matmul_z(2, 2)
+        matmul_out(1, 0, [0, 1, 2])
+        matmul_out(1, 1, [0, 1, 2])
+        mask_and_weigh(2, 1)
+        quantize_w(2, 0)
+        store_out(0, 2, "scalar")
+        store_out(0, 3, "scalar")
+        matmul_z(2, 3)
+        matmul_out(1, 2, [0, 1, 2])
+        matmul_out(1, 3, [0, 1, 2])
+        mask_and_weigh(2, 2)
+        quantize_w(2, 1)
+        matmul_z(3, 0)
+        out_pass(1, 3)
+        mask_and_weigh(2, 3)
+        quantize_w(2, 2)
+        matmul_z(3, 1)
+        mask_and_weigh(3, 0)
+        quantize_w(2, 3)
+        store_out(1, 0, "scalar")
+        store_out(1, 1, "scalar")
+        matmul_z(3, 2)
+        matmul_out(2, 0, [0, 1, 2])
+        matmul_out(2, 1, [0, 1, 2])
+        mask_and_weigh(3, 1)
+        quantize_w(3, 0)
+        matmul_z(3, 3)
+        for m in (0, 1):
+            matmul_out(2, m, [3])
+            matmul_out(2, m + 2, [0, 1, 2, 3])
+        mask_and_weigh(3, 2)
+        quantize_w(3, 1)
+        quantize_w(3, 2)
+        mask_and_weigh(3, 3)
+        store_pair(2, 0, "scalar")
+        store_pair(2, 1, "scalar")
+        store_out(1, 2, "scalar")
+        store_out(1, 3, "scalar")
+        for g in range(3):
+            out_pass(3, g)
+        quantize_w(3, 3)
         for m in tokens:
-            matmul_out(last, m, all_passes[3:])
-            store_out(last, m, "scalar" if m % 2 == 0 else "vector")
+            matmul_out(3, m, [3])
+            store_out(3, m, "scalar" if m % 2 == 0 else "vector")

@@ -25,7 +25,7 @@ TOKEN_TILES = M // P
 WIDTHS = (512, 512, 256, 256)
 STARTS = tuple(sum(WIDTHS[:c]) for c in range(len(WIDTHS)))
 B_LOADS = N // BANK
-RUN = 4
+RUN = 2
 
 
 def tile_sigmoid_masked_down_projection_s11_kernel(
@@ -106,12 +106,12 @@ def tile_sigmoid_masked_down_projection_s11_kernel(
             words = w_up_words.bitcast(I32)[:, :, g * 256 : (g + 1) * 256]
             nc.sync.dma_start(out=raw["up", g][:], in_=words.rearrange("a p w -> p a w"))
 
-        def load_up_scales(first, count):
+        def load_up_scales(first, count, queue):
             plane = sb.tile([P, D_PASSES, count * P], I32, name="up_scale_raw%d" % first)
-            nc.gpsimd.memset(plane[:], 0)
+            nc.vector.memset(plane[:], 0)
             rows = w_up_scales.bitcast(I32)[:, :, first * P : (first + count) * P]
             for q in range(4):
-                nc.sync.dma_start(
+                queue.dma_start(
                     out=plane[32 * q : 32 * q + 4, :, :],
                     in_=rows[:, 4 * q : 4 * q + 4, :].rearrange("a r w -> r a w"),
                 )
@@ -164,11 +164,12 @@ def tile_sigmoid_masked_down_projection_s11_kernel(
             grouped["x", m] = sb.tile([P, D], BF16, name="x_grouped", tag="x_grouped", bufs=2, align_bytes=64)
             gather_words(engine, grouped["x", m][:].bitcast(F32), banks["x", m])
 
-        def interleave_b(b, half):
+        def interleave_b(b, half, engine="vector"):
             grouped["b", b, half] = sb.tile([P, PACK * 256], BF16, name="b_grouped", tag="b_grouped", bufs=2, align_bytes=64)
-            nc.vector.tensor_copy(
-                out=grouped["b", b, half][:].rearrange("p (c i t) -> p c t i", i=4, t=PACK),
-                in_=raw["b", b][:, :, half * 256 : (half + 1) * 256].rearrange("p t (c i) -> p c t i", i=4),
+            copy_on(
+                engine,
+                grouped["b", b, half][:].rearrange("p (c i t) -> p c t i", i=4, t=PACK),
+                raw["b", b][:, :, half * 256 : (half + 1) * 256].rearrange("p t (c i) -> p c t i", i=4),
             )
 
         def quantize_b(b, half):
@@ -310,26 +311,27 @@ def tile_sigmoid_masked_down_projection_s11_kernel(
 
         identity = sb.tile([P, P], F32, name="identity")
         make_identity(nc, identity[:])
+        warm = sb.tile([P, 1], F32, name="warm")
+        nc.scalar.activation(out=warm[:], in_=identity[:, 0:1], func=ACT.Sigmoid)
 
         tokens = range(TOKEN_TILES)
+        load_up_scales(0, 2, nc.gpsimd)
         load_score_a(0)
         load_score_b(0)
         load_x(0)
         load_x(1)
         load_score_b(1)
-        load_up_scales(0, 1)
         load_up_codes(0)
         load_w(0, 0)
         load_score_a(1)
         load_x(2)
         load_x(3)
-        load_up_scales(1, 1)
         load_up_codes(1)
         load_w(1, 0)
         load_score_a(2)
         load_w(0, 1)
         load_score_a(3)
-        load_up_scales(2, 2)
+        load_up_scales(2, 2, nc.sync)
         load_up_codes(2)
         load_w(0, 2)
         load_score_b(2)
@@ -382,7 +384,8 @@ def tile_sigmoid_masked_down_projection_s11_kernel(
                 turn_a(u, "scalar", "scalar")
             gate(c, g)
             if u == 2:
-                turn_a(u, "scalar", "scalar")
+                turn_a(u, "scalar", "vector")
+                quantize_w(*units[u - 1])
             if 0 < hg and hg + 1 < F_PASSES:
                 sort_up(hg + 1)
             if u < 4:
@@ -406,7 +409,7 @@ def tile_sigmoid_masked_down_projection_s11_kernel(
                 interleave_b(2, 1)
                 quantize_b(2, 0)
                 quantize_b(2, 1)
-            if u <= 6:
+            if 2 < u <= 6:
                 quantize_w(*units[u - 1])
             multiply(c, g)
         quantize_w(1, 2)

@@ -17,15 +17,21 @@ ACT = mybir.ActivationFunctionType
 
 P = 128
 PACK = 4
+RUN = 4
 K_PASS = P * PACK
 BANK = 512
 D_PASSES = D // K_PASS
 F_PASSES = F // K_PASS
 TOKEN_TILES = M // P
+PANELS = N // BANK
 WIDTHS = (512, 512, 256, 256)
 STARTS = tuple(sum(WIDTHS[:c]) for c in range(len(WIDTHS)))
-B_LOADS = N // BANK
-RUN = 2
+UP_CODE_WORDS = K_PASS * 2 // 4
+UP_SCALE_WORDS = K_PASS // 4
+ROLE_BANKS = 4
+W_RAW_BUFS = 10
+NARROW_W_BUFS = 5
+RESULT_BUFS = 8
 
 
 def tile_sigmoid_masked_down_projection_s11_kernel(
@@ -37,150 +43,33 @@ def tile_sigmoid_masked_down_projection_s11_kernel(
         psum = ctx.enter_context(tc.psum_pool(name="psum", bufs=1))
         ctx.enter_context(tc.manual_schedule())
 
+        on_scalar = nc.scalar.copy
+        on_vector = nc.vector.tensor_copy
+
         raw = {}
+        grouped = {}
         codes = {}
         scales = {}
-        grouped = {}
         banks = {}
         mask = {}
-        turn = {"z": 0, "other": 0}
+        taken = {"z": 0, "other": 0}
 
         def take_bank(role, key):
-            index = turn[role] % 4 + (0 if role == "z" else 4)
-            turn[role] = turn[role] + 1
-            bank = psum.tile([P, BANK], F32, name="bank%d" % index, tag="bank%d" % index)
-            banks[key] = bank
-            return bank
+            index = taken[role] % ROLE_BANKS + (0 if role == "z" else ROLE_BANKS)
+            taken[role] = taken[role] + 1
+            banks[key] = psum.tile([P, BANK], F32, name="bank%d" % index, tag="bank%d" % index)
+            return banks[key]
 
-        def copy_on(engine, out_ap, in_ap):
-            if engine == "scalar":
-                nc.scalar.copy(out=out_ap, in_=in_ap)
-            else:
-                nc.vector.tensor_copy(out=out_ap, in_=in_ap)
-
-        def new_planes(key, tag, width, bufs):
-            codes[key] = sb.tile([P, width], U32, name=tag + "_codes", tag=tag + "_codes", bufs=bufs, align_bytes=64)
-            scales[key] = sb.tile([P, width], U8, name=tag + "_scales", tag=tag + "_scales", bufs=bufs, align_bytes=64)
-
-        def quantize_part(key, cols, source):
-            nc.vector.quantize_mx(out=codes[key][:, cols].bitcast(FP8X4), scales=scales[key][:, cols], in_=source)
+        def new_grouped(key, columns, bufs):
+            tag = key[0] + "_grouped"
+            grouped[key] = sb.tile([P, PACK * columns], BF16, name=tag, tag=tag, bufs=bufs, align_bytes=64)
+            return grouped[key]
 
         def quantize(key, tag, bufs):
             width = grouped[key].shape[1] // PACK
-            new_planes(key, tag, width, bufs)
-            quantize_part(key, slice(0, width), grouped[key][:])
-
-        def load_f_rows(key, source, g, cols, tag, bufs):
-            width = cols.stop - cols.start
-            raw[key] = sb.tile([P, PACK, width], BF16, name=tag, tag=tag, bufs=bufs)
-            rows = source[g * K_PASS : (g + 1) * K_PASS, cols].rearrange("(j t e) n -> e j t n", t=PACK, e=4)
-            for e in range(4):
-                nc.sync.dma_start(out=raw[key][e:P:4, :, :], in_=rows[e])
-
-        def load_score_a(g):
-            load_f_rows(("a", g), score_a, g, slice(0, R), "a_raw", F_PASSES)
-
-        def load_score_a_half(g, half):
-            raw["a", g, half] = sb.tile([P, 2, R], BF16, name="a_first", tag="a_first", bufs=2)
-            rows = score_a[g * K_PASS : (g + 1) * K_PASS, :].rearrange("(j t e) n -> e j t n", t=PACK, e=4)
-            for e in range(4):
-                nc.sync.dma_start(out=raw["a", g, half][e:P:4, :, :], in_=rows[e][:, 2 * half : 2 * half + 2, :])
-
-        def transpose_a_half(g, half):
-            transpose_pair(("a", g, half), raw["a", g, half][:].rearrange("p t k -> p (t k)").bitcast(F32))
-
-        def load_w(b, g):
-            load_f_rows(("w", b, g), w_down, g, slice(b * BANK, (b + 1) * BANK), "w_raw", 10)
-
-        def load_score_b(b):
-            raw["b", b] = sb.tile([P, PACK, BANK], BF16, name="b_raw", tag="b_raw", bufs=B_LOADS)
-            cols = score_b[:, b * BANK : (b + 1) * BANK]
-            nc.sync.dma_start(out=raw["b", b][:], in_=cols.rearrange("(p t) n -> p t n", t=PACK))
-
-        def load_x(m):
-            raw["x", m] = sb.tile([P, D], BF16, name="x_raw", tag="x_raw", bufs=TOKEN_TILES)
-            nc.sync.dma_start(out=raw["x", m][:], in_=x[m * P : (m + 1) * P, :])
-
-        def load_up_codes(g):
-            raw["up", g] = sb.tile([P, D_PASSES, 256], I32, name="up_raw", tag="up_raw", bufs=F_PASSES)
-            words = w_up_words.bitcast(I32)[:, :, g * 256 : (g + 1) * 256]
-            nc.sync.dma_start(out=raw["up", g][:], in_=words.rearrange("a p w -> p a w"))
-
-        def load_up_scales(first, count, queue):
-            plane = sb.tile([P, D_PASSES, count * P], I32, name="up_scale_raw%d" % first)
-            nc.vector.memset(plane[:], 0)
-            rows = w_up_scales.bitcast(I32)[:, :, first * P : (first + count) * P]
-            for q in range(4):
-                queue.dma_start(
-                    out=plane[32 * q : 32 * q + 4, :, :],
-                    in_=rows[:, 4 * q : 4 * q + 4, :].rearrange("a r w -> r a w"),
-                )
-            for g in range(count):
-                raw["up_scales", first + g] = plane[:, :, g * P : (g + 1) * P]
-
-        def sort_up(g):
-            codes["up", g] = sb.tile([P, D_PASSES * 1024], U8, name="up_codes", tag="up_codes", bufs=F_PASSES, align_bytes=64)
-            scales["up", g] = sb.tile([P, D_PASSES * 512], U8, name="up_scales", tag="up_scales", bufs=F_PASSES, align_bytes=64)
-            nc.vector.tensor_copy(
-                out=codes["up", g][:].bitcast(I32).rearrange("p (a t j w) -> p a t j w", a=D_PASSES, t=PACK, w=2),
-                in_=raw["up", g][:].rearrange("p a (j t w) -> p a t j w", t=PACK, w=2),
-            )
-            nc.vector.tensor_copy(
-                out=scales["up", g][:].bitcast(I32).rearrange("p (a t j) -> p a t j", a=D_PASSES, t=PACK),
-                in_=raw["up_scales", g].rearrange("p a (j t) -> p a t j", t=PACK),
-            )
-
-        def transpose_pair(key, words):
-            bank = take_bank("other", key)
-            for s in range(2):
-                for u in range(2):
-                    column = (2 * s + u) * P
-                    nc.tensor.transpose(
-                        bank[:, column : column + P], words[:, 256 * s + u : 256 * (s + 1) : 2], identity[:]
-                    )
-
-        def transpose_a(g):
-            words = raw["a", g][:].rearrange("p t k -> p (t k)").bitcast(F32)
-            for half in range(2):
-                transpose_pair(("a", g, half), words[:, half * BANK : (half + 1) * BANK])
-
-        def transpose_x(m):
-            transpose_pair(("x", m), raw["x", m][:].bitcast(F32))
-
-        def gather_words(engine, target, bank):
-            copy_on(
-                engine,
-                target.rearrange("p (s r u) -> p s r u", s=2, u=2),
-                bank[:].rearrange("p (s u r) -> p s r u", s=2, u=2),
-            )
-
-        def empty_a(g, half, engine):
-            if half == 0:
-                grouped["a", g] = sb.tile([P, PACK * K_PASS], BF16, name="a_grouped", tag="a_grouped", bufs=2, align_bytes=64)
-            words = grouped["a", g][:].bitcast(F32)
-            gather_words(engine, words[:, half * BANK : (half + 1) * BANK], banks["a", g, half])
-
-        def empty_x(m, engine):
-            grouped["x", m] = sb.tile([P, D], BF16, name="x_grouped", tag="x_grouped", bufs=2, align_bytes=64)
-            gather_words(engine, grouped["x", m][:].bitcast(F32), banks["x", m])
-
-        def interleave_b(b, half, engine="vector"):
-            grouped["b", b, half] = sb.tile([P, PACK * 256], BF16, name="b_grouped", tag="b_grouped", bufs=2, align_bytes=64)
-            copy_on(
-                engine,
-                grouped["b", b, half][:].rearrange("p (c i t) -> p c t i", i=4, t=PACK),
-                raw["b", b][:, :, half * 256 : (half + 1) * 256].rearrange("p t (c i) -> p c t i", i=4),
-            )
-
-        def quantize_b(b, half):
-            if half == 0:
-                new_planes(("b", b), "b", BANK, B_LOADS)
-            quantize_part(("b", b), slice(half * 256, (half + 1) * 256), grouped["b", b, half][:])
-
-        def quantize_a_half(g, half):
-            if half == 0:
-                new_planes(("a", g), "a", K_PASS, F_PASSES)
-            quantize_part(("a", g), slice(half * 256, (half + 1) * 256), grouped["a", g][:, half * 1024 : (half + 1) * 1024])
+            codes[key] = sb.tile([P, width], U32, name=tag + "_codes", tag=tag + "_codes", bufs=bufs, align_bytes=64)
+            scales[key] = sb.tile([P, width], U8, name=tag + "_scales", tag=tag + "_scales", bufs=bufs, align_bytes=64)
+            nc.vector.quantize_mx(out=codes[key][:].bitcast(FP8X4), scales=scales[key][:], in_=grouped[key][:])
 
         def mx(out_ap, stationary, s_cols, moving, m_cols, start, stop):
             nc.tensor.matmul_mx(
@@ -193,279 +82,348 @@ def tile_sigmoid_masked_down_projection_s11_kernel(
                 stop=stop,
             )
 
-        def matmul_h(g, m):
-            bank = take_bank("other", ("h", g, m))
+
+        def load_a(g):
+            raw["a", g] = sb.tile([P, RUN, R], BF16, name="a_raw", tag="a_raw", bufs=F_PASSES)
+            rows = score_a[g * K_PASS : (g + 1) * K_PASS, :]
+            nc.sync.dma_start(out=raw["a", g][:], in_=rows.rearrange("(p e) k -> p e k", e=RUN))
+
+        def load_w(panel, g):
+            raw["w", panel, g] = sb.tile([P, PACK, BANK], BF16, name="w_raw", tag="w_raw", bufs=W_RAW_BUFS)
+            rows = w_down[g * K_PASS : (g + 1) * K_PASS, panel * BANK : (panel + 1) * BANK]
+            rows = rows.rearrange("(j t e) n -> t j e n", t=PACK, e=RUN)
             for t in range(PACK):
-                for a in range(D_PASSES):
-                    column = (a * PACK + t) * P
-                    nc.tensor.matmul_mx(
-                        out=bank[:, t * P : (t + 1) * P],
-                        lhsT=codes["up", g][:, 2 * column : 2 * (column + P)].bitcast(FP4X4),
-                        lhsT_scale=scales["up", g][:, column : column + P],
-                        rhs=codes["x", m][:, a * P : (a + 1) * P].bitcast(FP8X4),
-                        rhs_scale=scales["x", m][:, a * P : (a + 1) * P],
-                        start=(a == 0),
-                        stop=(a == D_PASSES - 1),
+                nc.sync.dma_start(out=raw["w", panel, g][:, t, :], in_=rows[t])
+
+        def load_b(panel):
+            raw["b", panel] = sb.tile([P, PACK, BANK], BF16, name="b_raw", tag="b_raw", bufs=PANELS)
+            cols = score_b[:, panel * BANK : (panel + 1) * BANK]
+            nc.sync.dma_start(out=raw["b", panel][:], in_=cols.rearrange("(p t) n -> p t n", t=PACK))
+
+        def load_x(m):
+            raw["x", m] = sb.tile([P, D], BF16, name="x_raw", tag="x_raw", bufs=TOKEN_TILES)
+            nc.sync.dma_start(out=raw["x", m][:], in_=x[m * P : (m + 1) * P, :])
+
+        def load_up(first, count):
+            plane = sb.tile([P, D_PASSES, count * UP_SCALE_WORDS], I32, name="up_scale_raw%d" % first)
+            raw["up_scales", first] = plane
+            nc.vector.memset(plane[:], 0)
+            rows = w_up_scales.bitcast(I32)[:, :, first * UP_SCALE_WORDS : (first + count) * UP_SCALE_WORDS]
+            for q in range(4):
+                nc.sync.dma_start(
+                    out=plane[32 * q : 32 * q + 4, :, :],
+                    in_=rows[:, 4 * q : 4 * q + 4, :].rearrange("a r w -> r a w"),
+                )
+            raw["up", first] = sb.tile([P, D_PASSES, count * UP_CODE_WORDS], I32, name="up_raw%d" % first)
+            words = w_up_words.bitcast(I32)[:, :, first * UP_CODE_WORDS : (first + count) * UP_CODE_WORDS]
+            nc.sync.dma_start(out=raw["up", first][:], in_=words.rearrange("a p w -> p a w"))
+
+
+        def sort_up(first, count):
+            sorted_codes = sb.tile([P, D_PASSES, count, 2 * K_PASS], U8, name="up_codes%d" % first, align_bytes=64)
+            sorted_scales = sb.tile([P, D_PASSES, count, K_PASS], U8, name="up_scales%d" % first, align_bytes=64)
+            nc.vector.tensor_copy(
+                out=sorted_codes[:].bitcast(I32).rearrange("p a g (t j w) -> p (a g) t j w", t=PACK, w=2),
+                in_=raw["up", first][:].rearrange("p a (g j t w) -> p (a g) t j w", g=count, t=PACK, w=2),
+            )
+            nc.vector.tensor_copy(
+                out=sorted_scales[:].bitcast(I32).rearrange("p a g (t j) -> p (a g) t j", t=PACK),
+                in_=raw["up_scales", first][:].rearrange("p a (g j t) -> p (a g) t j", g=count, t=PACK),
+            )
+            for g in range(count):
+                codes["up", first + g] = sorted_codes[:, :, g, :]
+                scales["up", first + g] = sorted_scales[:, :, g, :]
+
+        def transpose_words(key, words):
+            bank = take_bank("other", key)
+            for s in range(2):
+                for u in range(2):
+                    column = (2 * s + u) * P
+                    nc.tensor.transpose(
+                        bank[:, column : column + P], words[:, 256 * s + u : 256 * (s + 1) : 2], identity[:]
                     )
+            return bank
 
-        def relu_h(g, m, engine):
-            if m == 0:
-                grouped["h", g] = sb.tile([P, PACK * M], BF16, name="h_grouped", tag="h_grouped", bufs=2, align_bytes=64)
-            target = grouped["h", g][:, m * BANK : (m + 1) * BANK].rearrange("p (r t) -> p r t", t=PACK)
-            sums = banks["h", g, m][:].rearrange("p (t r) -> p r t", t=PACK)
-            if engine == "scalar":
-                nc.scalar.activation(out=target, in_=sums, func=ACT.Relu)
-            else:
-                nc.vector.tensor_scalar_max(target, sums, 0.0)
+        def turn_a(g, copy):
+            words = raw["a", g][:].rearrange("p e k -> p (e k)").bitcast(F32)
+            turned = [transpose_words(("a", g, h), words[:, h * BANK : (h + 1) * BANK]) for h in range(2)]
+            target = new_grouped(("a", g), K_PASS, 2)[:].bitcast(F32)
+            target = target.rearrange("p (t j h e u) -> p h t j e u", t=PACK, h=2, e=2, u=2)
+            for h in range(2):
+                copy(out=target[:, h], in_=turned[h][:].rearrange("p (e u j t) -> p t j e u", e=2, u=2, t=PACK))
 
-        def matmul_z(c, g):
-            width = WIDTHS[c]
-            per_bank = BANK // width
-            b, first = divmod(STARTS[c], BANK)
-            for t in range(PACK):
-                if t % per_bank == 0:
-                    bank = take_bank("z", ("z", c, g, t // per_bank))
-                column = (t % per_bank) * width
-                mx(bank[:, column : column + width], ("a", g), slice(t * P, (t + 1) * P), ("b", b), slice(first, first + width), True, True)
-
-        def sigmoid_z(c, g):
-            mask[c, g] = sb.tile([P, PACK * WIDTHS[c]], F32, name="mask", tag="mask", bufs=3)
-            for s in range(PACK * WIDTHS[c] // BANK):
-                nc.scalar.activation(out=mask[c, g][:, s * BANK : (s + 1) * BANK], in_=banks["z", c, g, s][:], func=ACT.Sigmoid)
-
-        def multiply(c, g):
-            width = WIDTHS[c]
-            grouped["w", c, g] = sb.tile([P, PACK * width], BF16, name="w_grouped", tag="w_grouped", bufs=3, align_bytes=64)
-            b, first = divmod(STARTS[c], BANK)
-            weights = raw["w", b, g][:, :, first : first + width]
-            nc.vector.tensor_tensor(
-                out=grouped["w", c, g][:].rearrange("p (c i t) -> p c t i", i=RUN, t=PACK),
-                in0=mask[c, g][:].rearrange("p (t c i) -> p c t i", t=PACK, i=RUN),
-                in1=weights.rearrange("p t (c i) -> p c t i", i=RUN),
-                op=mybir.AluOpType.mult,
+        def turn_x(m):
+            bank = transpose_words(("x", m), raw["x", m][:].bitcast(F32))
+            if m % 2 == 0:
+                new_grouped(("x", m // 2), 2 * D_PASSES * P, 1)
+            target = grouped["x", m // 2][:].bitcast(F32)[:, m % 2 * BANK : (m % 2 + 1) * BANK]
+            on_scalar(
+                out=target.rearrange("p (a r u) -> p a r u", a=D_PASSES, u=2),
+                in_=bank[:].rearrange("p (a u r) -> p a r u", a=D_PASSES, u=2),
             )
 
-        def quantize_w(c, g):
-            quantize(("w", c, g), "w%d" % WIDTHS[c], 8 if WIDTHS[c] == BANK else 5)
+        def interleave_b(panel):
+            on_vector(
+                out=new_grouped(("b", panel), BANK, 1)[:].rearrange("p (c i t) -> p c t i", i=4, t=PACK),
+                in_=raw["b", panel][:].rearrange("p t (c i) -> p c t i", i=4),
+            )
 
-        def matmul_out(c, m, passes):
-            width = WIDTHS[c]
-            shared = c == 2 and m >= 2
-            if passes[0] == 0:
-                if shared:
-                    banks["out", c, m] = banks["out", c, m - 2]
-                else:
-                    take_bank("z" if c == 3 else "other", ("out", c, m))
-            first = width if shared else 0
-            for g in passes:
-                mx(banks["out", c, m][:, first : first + width], ("h", g), slice(m * P, (m + 1) * P), ("w", c, g), slice(0, width), g == 0, g == F_PASSES - 1)
-
-        def store_out(c, m, engine):
-            width = WIDTHS[c]
-            result = sb.tile([P, width], F32, name="result", tag="result", bufs=8)
-            copy_on(engine, result[:], banks["out", c, m][:, 0:width])
-            nc.sync.dma_start(out=out[m * P : (m + 1) * P, STARTS[c] : STARTS[c] + width], in_=result[:])
-
-        def store_pair(c, m, engine):
-            width = WIDTHS[c]
-            result = sb.tile([P, 2 * width], F32, name="result", tag="result", bufs=8)
-            copy_on(engine, result[:], banks["out", c, m][:])
-            rows = out[:, STARTS[c] : STARTS[c] + width].rearrange("(h m p) n -> m p h n", h=2, p=P)
-            nc.sync.dma_start(out=rows[m], in_=result[:].rearrange("p (h n) -> p h n", h=2))
-
-        def hidden(g, m, engine="scalar"):
-            matmul_h(g, m)
-            relu_h(g, m, engine)
-
-        def turn_a(g, first_engine, second_engine):
-            transpose_a(g)
-            empty_a(g, 0, first_engine)
-            empty_a(g, 1, second_engine)
-
-        def gate(c, g):
-            matmul_z(c, g)
-            sigmoid_z(c, g)
-
-        def prepare_b(b):
-            interleave_b(b, 0)
-            interleave_b(b, 1)
-            quantize_b(b, 0)
-            quantize_b(b, 1)
-
-        def quantize_x(m):
-            quantize(("x", m), "x", TOKEN_TILES)
+        def quantize_x(pair):
+            quantize(("x", pair), "x", TOKEN_TILES // 2)
 
         def quantize_a(g):
             quantize(("a", g), "a", F_PASSES)
 
+        def quantize_b(panel):
+            quantize(("b", panel), "b", PANELS)
+
+
+        def hidden(g, m):
+            bank = take_bank("other", ("h", g, m))
+            for t in range(PACK):
+                for a in range(D_PASSES):
+                    x_first = (m % 2 * D_PASSES + a) * P
+                    nc.tensor.matmul_mx(
+                        out=bank[:, t * P : (t + 1) * P],
+                        lhsT=codes["up", g][:, a, 2 * t * P : 2 * (t + 1) * P].bitcast(FP4X4),
+                        lhsT_scale=scales["up", g][:, a, t * P : (t + 1) * P],
+                        rhs=codes["x", m // 2][:, x_first : x_first + P].bitcast(FP8X4),
+                        rhs_scale=scales["x", m // 2][:, x_first : x_first + P],
+                        start=(a == 0),
+                        stop=(a == D_PASSES - 1),
+                    )
+            if m == 0:
+                new_grouped(("h", g), M, 2)
+            nc.scalar.activation(
+                out=grouped["h", g][:, m * PACK * P : (m + 1) * PACK * P].rearrange("p (r t) -> p r t", t=PACK),
+                in_=bank[:].rearrange("p (t r) -> p r t", t=PACK),
+                func=ACT.Relu,
+            )
+
         def quantize_h(g):
             quantize(("h", g), "h", F_PASSES)
 
-        def out_pass(c, g):
-            for m in range(TOKEN_TILES):
-                matmul_out(c, m, [g])
 
-        def store_chunk(c):
-            for m in range(TOKEN_TILES):
-                store_out(c, m, "scalar")
+        def scores(c, g):
+            width = WIDTHS[c]
+            per_bank = BANK // width
+            panel, first = divmod(STARTS[c], BANK)
+            for t in range(PACK):
+                if t % per_bank == 0:
+                    bank = take_bank("z", ("z", c, g, t // per_bank))
+                column = (t % per_bank) * width
+                a_cols = slice(t * P, (t + 1) * P)
+                mx(bank[:, column : column + width], ("a", g), a_cols, ("b", panel), slice(first, first + width), True, True)
+
+        def sigmoid(c, g):
+            mask[c, g] = sb.tile([P, PACK * WIDTHS[c]], F32, name="mask", tag="mask", bufs=3)
+            for s in range(PACK * WIDTHS[c] // BANK):
+                nc.scalar.activation(
+                    out=mask[c, g][:, s * BANK : (s + 1) * BANK], in_=banks["z", c, g, s][:], func=ACT.Sigmoid
+                )
+
+        def multiply(c, g):
+            width = WIDTHS[c]
+            panel, first = divmod(STARTS[c], BANK)
+            nc.vector.tensor_tensor(
+                out=new_grouped(("w", c, g), width, 3)[:].rearrange("p (c i t) -> p c t i", i=2, t=PACK),
+                in0=mask[c, g][:].rearrange("p (t c i) -> p c t i", t=PACK, i=2),
+                in1=raw["w", panel, g][:, :, first : first + width].rearrange("p t (c i) -> p c t i", i=2),
+                op=mybir.AluOpType.mult,
+            )
+
+        def quantize_w(c, g):
+            quantize(("w", c, g), "w%d" % WIDTHS[c], 2 * F_PASSES if WIDTHS[c] == BANK else NARROW_W_BUFS)
+
+        def gate(c, g):
+            scores(c, g)
+            sigmoid(c, g)
+
+        def weigh(c, g):
+            sigmoid(c, g)
+            multiply(c, g)
+
+
+        def product(c, m, passes, first=0):
+            width = WIDTHS[c]
+            for g in passes:
+                target = banks["out", c, m][:, first : first + width]
+                mx(target, ("h", g), slice(m * P, (m + 1) * P), ("w", c, g), slice(0, width), g == 0, g == F_PASSES - 1)
+
+        def open_product(c, m, passes, role):
+            take_bank(role, ("out", c, m))
+            product(c, m, passes)
+
+        def store(c, m, copy):
+            width = WIDTHS[c]
+            result = sb.tile([P, width], F32, name="result", tag="result", bufs=RESULT_BUFS)
+            copy(out=result[:], in_=banks["out", c, m][:, 0:width])
+            nc.sync.dma_start(out=out[m * P : (m + 1) * P, STARTS[c] : STARTS[c] + width], in_=result[:])
+
+        def store_pair(c, m):
+            width = WIDTHS[c]
+            result = sb.tile([P, 2 * width], F32, name="result", tag="result", bufs=RESULT_BUFS)
+            on_scalar(out=result[:], in_=banks["out", c, m][:])
+            rows = out[:, STARTS[c] : STARTS[c] + width].rearrange("(h m p) n -> m p h n", h=2, p=P)
+            nc.sync.dma_start(out=rows[m], in_=result[:].rearrange("p (h n) -> p h n", h=2))
+
+        tokens = range(TOKEN_TILES)
+        early = range(F_PASSES - 1)
+        final = [F_PASSES - 1]
 
         identity = sb.tile([P, P], F32, name="identity")
         make_identity(nc, identity[:])
         warm = sb.tile([P, 1], F32, name="warm")
         nc.scalar.activation(out=warm[:], in_=identity[:, 0:1], func=ACT.Sigmoid)
 
-        tokens = range(TOKEN_TILES)
-        load_up_scales(0, 2, nc.gpsimd)
-        load_score_a(0)
-        load_score_b(0)
+        load_a(0)
+        load_b(0)
         load_x(0)
         load_x(1)
-        load_score_b(1)
-        load_up_codes(0)
+        load_b(1)
+        load_up(0, 1)
         load_w(0, 0)
-        load_score_a(1)
+        load_a(1)
         load_x(2)
         load_x(3)
-        load_up_codes(1)
+        load_up(1, 1)
+        load_a(2)
         load_w(1, 0)
-        load_score_a(2)
         load_w(0, 1)
-        load_score_a(3)
-        load_up_scales(2, 2, nc.sync)
-        load_up_codes(2)
+        load_a(3)
+        load_up(2, 2)
         load_w(0, 2)
-        load_score_b(2)
-        load_up_codes(3)
+        load_b(2)
         load_w(0, 3)
-        load_w(1, 1)
-        load_w(1, 2)
-        load_w(1, 3)
+        for g in range(1, F_PASSES):
+            load_w(1, g)
         load_w(2, 0)
         load_w(2, 1)
 
-        turn_a(0, "scalar", "scalar")
-        interleave_b(0, 0)
-        quantize_a_half(0, 0)
-        interleave_b(0, 1)
-        quantize_b(0, 0)
-        quantize_b(0, 1)
-        quantize_a_half(0, 1)
-        transpose_x(0)
-        empty_x(0, "scalar")
-        transpose_x(1)
-        empty_x(1, "scalar")
+        turn_a(0, on_scalar)
+        interleave_b(0)
+        quantize_a(0)
+        quantize_b(0)
+        turn_x(0)
+        turn_x(1)
         gate(0, 0)
+        interleave_b(1)
         quantize_x(0)
-        prepare_b(1)
+        quantize_b(1)
         gate(1, 0)
-        quantize_x(1)
-        sort_up(0)
+        sort_up(0, 1)
         multiply(0, 0)
         hidden(0, 0)
-        turn_a(1, "vector", "scalar")
+        turn_a(1, on_vector)
         hidden(0, 1)
-        transpose_x(2)
-        empty_x(2, "scalar")
-        transpose_x(3)
-        empty_x(3, "scalar")
-        quantize_w(0, 0)
+        turn_x(2)
+        turn_x(3)
+        sort_up(1, 1)
         quantize_a(1)
-        sort_up(1)
-        quantize_x(2)
-        quantize_x(3)
+        quantize_w(0, 0)
+        quantize_x(1)
         multiply(1, 0)
         load_w(2, 2)
         load_w(2, 3)
-        units = [(0, 0), (1, 0), (0, 1), (0, 2), (0, 3), (1, 1), (1, 2), (1, 3)] + [(c, g) for c in (2, 3) for g in range(F_PASSES)]
-        for u in range(2, 8):
-            c, g = units[u]
-            hg = u - 2
-            if u == 3:
-                turn_a(u, "scalar", "scalar")
-            gate(c, g)
-            if u == 2:
-                turn_a(u, "scalar", "vector")
-                quantize_w(*units[u - 1])
-            if 0 < hg and hg + 1 < F_PASSES:
-                sort_up(hg + 1)
-            if u < 4:
-                quantize_a(u)
-            if 0 < hg <= F_PASSES:
-                quantize_h(hg - 1)
-            if hg < F_PASSES:
-                hidden(hg, 2)
-                hidden(hg, 3)
-            if hg + 1 < F_PASSES:
-                hidden(hg + 1, 0)
-                hidden(hg + 1, 1)
-            if u == 6:
-                out_pass(0, 0)
-                out_pass(0, 1)
-            if u == 7:
-                out_pass(0, 2)
-            if u == 4:
-                interleave_b(2, 0)
-            if u == 5:
-                interleave_b(2, 1)
-                quantize_b(2, 0)
-                quantize_b(2, 1)
-            if 2 < u <= 6:
-                quantize_w(*units[u - 1])
-            multiply(c, g)
+
+        gate(0, 1)
+        turn_a(2, on_scalar)
+        quantize_w(1, 0)
+        quantize_a(2)
+        for g, m in ((0, 2), (0, 3), (1, 0), (1, 1)):
+            hidden(g, m)
+        multiply(0, 1)
+
+        turn_a(3, on_scalar)
+        gate(0, 2)
+        sort_up(2, 2)
+        quantize_a(3)
+        quantize_h(0)
+        for g, m in ((1, 2), (1, 3), (2, 0), (2, 1)):
+            hidden(g, m)
+        quantize_w(0, 1)
+        multiply(0, 2)
+
+        gate(0, 3)
+        quantize_h(1)
+        for g, m in ((2, 2), (2, 3), (3, 0), (3, 1)):
+            hidden(g, m)
+        interleave_b(2)
+        quantize_w(0, 2)
+        multiply(0, 3)
+
+        gate(1, 1)
+        quantize_h(2)
+        hidden(3, 2)
+        hidden(3, 3)
+        quantize_b(2)
+        quantize_w(0, 3)
+        multiply(1, 1)
+
+        gate(1, 2)
+        quantize_h(3)
+        for m in tokens:
+            open_product(0, m, [0], "other")
+        for m in tokens:
+            product(0, m, [1])
+        quantize_w(1, 1)
+        multiply(1, 2)
+
+        gate(1, 3)
+        for m in tokens:
+            product(0, m, [2])
+        multiply(1, 3)
         quantize_w(1, 2)
 
-        def mask_and_weigh(c, g):
-            sigmoid_z(c, g)
-            multiply(c, g)
-
-        matmul_z(2, 0)
-        out_pass(0, 3)
-        matmul_z(2, 1)
-        mask_and_weigh(2, 0)
+        scores(2, 0)
+        for m in tokens:
+            product(0, m, final)
+        scores(2, 1)
+        weigh(2, 0)
         quantize_w(1, 3)
-        store_out(0, 0, "scalar")
-        store_out(0, 1, "scalar")
-        matmul_z(2, 2)
-        matmul_out(1, 0, [0, 1, 2])
-        matmul_out(1, 1, [0, 1, 2])
-        mask_and_weigh(2, 1)
-        quantize_w(2, 0)
-        store_out(0, 2, "scalar")
-        store_out(0, 3, "scalar")
-        matmul_z(2, 3)
-        matmul_out(1, 2, [0, 1, 2])
-        matmul_out(1, 3, [0, 1, 2])
-        mask_and_weigh(2, 2)
-        quantize_w(2, 1)
-        matmul_z(3, 0)
-        out_pass(1, 3)
-        mask_and_weigh(2, 3)
+        for step in range(2):
+            pair = (2 * step, 2 * step + 1)
+            for m in pair:
+                store(0, m, on_scalar)
+            scores(2, step + 2)
+            for m in pair:
+                open_product(1, m, early, "other")
+            weigh(2, step + 1)
+            quantize_w(2, step)
+        scores(3, 0)
+        for m in tokens:
+            product(1, m, final)
+        weigh(2, 3)
         quantize_w(2, 2)
-        matmul_z(3, 1)
-        mask_and_weigh(3, 0)
+        scores(3, 1)
+        weigh(3, 0)
         quantize_w(2, 3)
-        store_out(1, 0, "scalar")
-        store_out(1, 1, "scalar")
-        matmul_z(3, 2)
-        matmul_out(2, 0, [0, 1, 2])
-        matmul_out(2, 1, [0, 1, 2])
-        mask_and_weigh(3, 1)
+        store(1, 0, on_scalar)
+        store(1, 1, on_scalar)
+        scores(3, 2)
+        open_product(2, 0, early, "other")
+        open_product(2, 1, early, "other")
+        weigh(3, 1)
         quantize_w(3, 0)
-        matmul_z(3, 3)
-        for m in (0, 1):
-            matmul_out(2, m, [3])
-            matmul_out(2, m + 2, [0, 1, 2, 3])
-        mask_and_weigh(3, 2)
+        scores(3, 3)
+        for m in range(2):
+            product(2, m, final)
+            banks["out", 2, m + 2] = banks["out", 2, m]
+            product(2, m + 2, range(F_PASSES), first=WIDTHS[2])
+        weigh(3, 2)
         quantize_w(3, 1)
         quantize_w(3, 2)
-        mask_and_weigh(3, 3)
-        store_pair(2, 0, "scalar")
-        store_pair(2, 1, "scalar")
-        store_out(1, 2, "scalar")
-        store_out(1, 3, "scalar")
-        for g in range(3):
-            out_pass(3, g)
+        weigh(3, 3)
+        store_pair(2, 0)
+        store_pair(2, 1)
+        store(1, 2, on_scalar)
+        store(1, 3, on_scalar)
+        for m in tokens:
+            open_product(3, m, [0], "z")
+        for g in early[1:]:
+            for m in tokens:
+                product(3, m, [g])
         quantize_w(3, 3)
         for m in tokens:
-            matmul_out(3, m, [3])
-            store_out(3, m, "scalar" if m % 2 == 0 else "vector")
+            product(3, m, final)
+            store(3, m, on_scalar if m % 2 == 0 else on_vector)

from contextlib import ExitStack

import concourse.mybir as mybir
from concourse.masks import make_identity

M, D, F, R, N = 512, 1024, 2048, 512, 1536
FLOPS = 2 * (M * D * F + F * R * N + M * F * N)

F32 = mybir.dt.float32
BF16 = mybir.dt.bfloat16
I32 = mybir.dt.int32
U32 = mybir.dt.uint32
U8 = mybir.dt.uint8
FP8X4 = mybir.dt.float8_e4m3fn_x4
FP4X4 = mybir.dt.float4_e2m1fn_x4
ACT = mybir.ActivationFunctionType

P = 128
PACK = 4
RUN = 4
K_PASS = P * PACK
BANK = 512
D_PASSES = D // K_PASS
F_PASSES = F // K_PASS
TOKEN_TILES = M // P
PANELS = N // BANK
WIDTHS = (512, 512, 256, 256)
STARTS = tuple(sum(WIDTHS[:c]) for c in range(len(WIDTHS)))
UP_CODE_WORDS = K_PASS * 2 // 4
UP_SCALE_WORDS = K_PASS // 4
ROLE_BANKS = 4
W_RAW_BUFS = 10
NARROW_W_BUFS = 5
RESULT_BUFS = 8


def tile_sigmoid_masked_down_projection_s11_kernel(
    tc, x, w_up_words, w_up_scales, score_a, score_b, w_down, out
):
    nc = tc.nc
    with ExitStack() as ctx:
        sb = ctx.enter_context(tc.tile_pool(name="sb", bufs=1))
        psum = ctx.enter_context(tc.psum_pool(name="psum", bufs=1))
        ctx.enter_context(tc.manual_schedule())

        on_scalar = nc.scalar.copy
        on_vector = nc.vector.tensor_copy

        raw = {}
        grouped = {}
        codes = {}
        scales = {}
        banks = {}
        mask = {}
        taken = {"z": 0, "other": 0}

        def take_bank(role, key):
            index = taken[role] % ROLE_BANKS + (0 if role == "z" else ROLE_BANKS)
            taken[role] = taken[role] + 1
            banks[key] = psum.tile([P, BANK], F32, name="bank%d" % index, tag="bank%d" % index)
            return banks[key]

        def new_grouped(key, columns, bufs):
            tag = key[0] + "_grouped"
            grouped[key] = sb.tile([P, PACK * columns], BF16, name=tag, tag=tag, bufs=bufs, align_bytes=64)
            return grouped[key]

        def quantize(key, tag, bufs):
            width = grouped[key].shape[1] // PACK
            codes[key] = sb.tile([P, width], U32, name=tag + "_codes", tag=tag + "_codes", bufs=bufs, align_bytes=64)
            scales[key] = sb.tile([P, width], U8, name=tag + "_scales", tag=tag + "_scales", bufs=bufs, align_bytes=64)
            nc.vector.quantize_mx(out=codes[key][:].bitcast(FP8X4), scales=scales[key][:], in_=grouped[key][:])

        def mx(out_ap, stationary, s_cols, moving, m_cols, start, stop):
            nc.tensor.matmul_mx(
                out=out_ap,
                lhsT=codes[stationary][:, s_cols].bitcast(FP8X4),
                lhsT_scale=scales[stationary][:, s_cols],
                rhs=codes[moving][:, m_cols].bitcast(FP8X4),
                rhs_scale=scales[moving][:, m_cols],
                start=start,
                stop=stop,
            )


        def load_a(g):
            raw["a", g] = sb.tile([P, RUN, R], BF16, name="a_raw", tag="a_raw", bufs=F_PASSES)
            rows = score_a[g * K_PASS : (g + 1) * K_PASS, :]
            nc.sync.dma_start(out=raw["a", g][:], in_=rows.rearrange("(p e) k -> p e k", e=RUN))

        def load_w(panel, g):
            raw["w", panel, g] = sb.tile([P, PACK, BANK], BF16, name="w_raw", tag="w_raw", bufs=W_RAW_BUFS)
            rows = w_down[g * K_PASS : (g + 1) * K_PASS, panel * BANK : (panel + 1) * BANK]
            rows = rows.rearrange("(j t e) n -> t j e n", t=PACK, e=RUN)
            for t in range(PACK):
                nc.sync.dma_start(out=raw["w", panel, g][:, t, :], in_=rows[t])

        def load_b(panel):
            raw["b", panel] = sb.tile([P, PACK, BANK], BF16, name="b_raw", tag="b_raw", bufs=PANELS)
            cols = score_b[:, panel * BANK : (panel + 1) * BANK]
            nc.sync.dma_start(out=raw["b", panel][:], in_=cols.rearrange("(p t) n -> p t n", t=PACK))

        def load_x(m):
            raw["x", m] = sb.tile([P, D], BF16, name="x_raw", tag="x_raw", bufs=TOKEN_TILES)
            nc.sync.dma_start(out=raw["x", m][:], in_=x[m * P : (m + 1) * P, :])

        def load_up(first, count):
            plane = sb.tile([P, D_PASSES, count * UP_SCALE_WORDS], I32, name="up_scale_raw%d" % first)
            raw["up_scales", first] = plane
            nc.vector.memset(plane[:], 0)
            rows = w_up_scales.bitcast(I32)[:, :, first * UP_SCALE_WORDS : (first + count) * UP_SCALE_WORDS]
            for q in range(4):
                nc.sync.dma_start(
                    out=plane[32 * q : 32 * q + 4, :, :],
                    in_=rows[:, 4 * q : 4 * q + 4, :].rearrange("a r w -> r a w"),
                )
            raw["up", first] = sb.tile([P, D_PASSES, count * UP_CODE_WORDS], I32, name="up_raw%d" % first)
            words = w_up_words.bitcast(I32)[:, :, first * UP_CODE_WORDS : (first + count) * UP_CODE_WORDS]
            nc.sync.dma_start(out=raw["up", first][:], in_=words.rearrange("a p w -> p a w"))


        def sort_up(first, count):
            sorted_codes = sb.tile([P, D_PASSES, count, 2 * K_PASS], U8, name="up_codes%d" % first, align_bytes=64)
            sorted_scales = sb.tile([P, D_PASSES, count, K_PASS], U8, name="up_scales%d" % first, align_bytes=64)
            nc.vector.tensor_copy(
                out=sorted_codes[:].bitcast(I32).rearrange("p a g (t j w) -> p (a g) t j w", t=PACK, w=2),
                in_=raw["up", first][:].rearrange("p a (g j t w) -> p (a g) t j w", g=count, t=PACK, w=2),
            )
            nc.vector.tensor_copy(
                out=sorted_scales[:].bitcast(I32).rearrange("p a g (t j) -> p (a g) t j", t=PACK),
                in_=raw["up_scales", first][:].rearrange("p a (g j t) -> p (a g) t j", g=count, t=PACK),
            )
            for g in range(count):
                codes["up", first + g] = sorted_codes[:, :, g, :]
                scales["up", first + g] = sorted_scales[:, :, g, :]

        def transpose_words(key, words):
            bank = take_bank("other", key)
            for s in range(2):
                for u in range(2):
                    column = (2 * s + u) * P
                    nc.tensor.transpose(
                        bank[:, column : column + P], words[:, 256 * s + u : 256 * (s + 1) : 2], identity[:]
                    )
            return bank

        def turn_a(g, copy):
            words = raw["a", g][:].rearrange("p e k -> p (e k)").bitcast(F32)
            turned = [transpose_words(("a", g, h), words[:, h * BANK : (h + 1) * BANK]) for h in range(2)]
            target = new_grouped(("a", g), K_PASS, 2)[:].bitcast(F32)
            target = target.rearrange("p (t j h e u) -> p h t j e u", t=PACK, h=2, e=2, u=2)
            for h in range(2):
                copy(out=target[:, h], in_=turned[h][:].rearrange("p (e u j t) -> p t j e u", e=2, u=2, t=PACK))

        def turn_x(m):
            bank = transpose_words(("x", m), raw["x", m][:].bitcast(F32))
            if m % 2 == 0:
                new_grouped(("x", m // 2), 2 * D_PASSES * P, 1)
            target = grouped["x", m // 2][:].bitcast(F32)[:, m % 2 * BANK : (m % 2 + 1) * BANK]
            on_scalar(
                out=target.rearrange("p (a r u) -> p a r u", a=D_PASSES, u=2),
                in_=bank[:].rearrange("p (a u r) -> p a r u", a=D_PASSES, u=2),
            )

        def interleave_b(panel):
            on_vector(
                out=new_grouped(("b", panel), BANK, 1)[:].rearrange("p (c i t) -> p c t i", i=4, t=PACK),
                in_=raw["b", panel][:].rearrange("p t (c i) -> p c t i", i=4),
            )

        def quantize_x(pair):
            quantize(("x", pair), "x", TOKEN_TILES // 2)

        def quantize_a(g):
            quantize(("a", g), "a", F_PASSES)

        def quantize_b(panel):
            quantize(("b", panel), "b", PANELS)


        def hidden(g, m):
            bank = take_bank("other", ("h", g, m))
            for t in range(PACK):
                for a in range(D_PASSES):
                    x_first = (m % 2 * D_PASSES + a) * P
                    nc.tensor.matmul_mx(
                        out=bank[:, t * P : (t + 1) * P],
                        lhsT=codes["up", g][:, a, 2 * t * P : 2 * (t + 1) * P].bitcast(FP4X4),
                        lhsT_scale=scales["up", g][:, a, t * P : (t + 1) * P],
                        rhs=codes["x", m // 2][:, x_first : x_first + P].bitcast(FP8X4),
                        rhs_scale=scales["x", m // 2][:, x_first : x_first + P],
                        start=(a == 0),
                        stop=(a == D_PASSES - 1),
                    )
            if m == 0:
                new_grouped(("h", g), M, 2)
            nc.scalar.activation(
                out=grouped["h", g][:, m * PACK * P : (m + 1) * PACK * P].rearrange("p (r t) -> p r t", t=PACK),
                in_=bank[:].rearrange("p (t r) -> p r t", t=PACK),
                func=ACT.Relu,
            )

        def quantize_h(g):
            quantize(("h", g), "h", F_PASSES)


        def scores(c, g):
            width = WIDTHS[c]
            per_bank = BANK // width
            panel, first = divmod(STARTS[c], BANK)
            for t in range(PACK):
                if t % per_bank == 0:
                    bank = take_bank("z", ("z", c, g, t // per_bank))
                column = (t % per_bank) * width
                a_cols = slice(t * P, (t + 1) * P)
                mx(bank[:, column : column + width], ("a", g), a_cols, ("b", panel), slice(first, first + width), True, True)

        def sigmoid(c, g):
            mask[c, g] = sb.tile([P, PACK * WIDTHS[c]], F32, name="mask", tag="mask", bufs=3)
            for s in range(PACK * WIDTHS[c] // BANK):
                nc.scalar.activation(
                    out=mask[c, g][:, s * BANK : (s + 1) * BANK], in_=banks["z", c, g, s][:], func=ACT.Sigmoid
                )

        def multiply(c, g):
            width = WIDTHS[c]
            panel, first = divmod(STARTS[c], BANK)
            nc.vector.tensor_tensor(
                out=new_grouped(("w", c, g), width, 3)[:].rearrange("p (c i t) -> p c t i", i=2, t=PACK),
                in0=mask[c, g][:].rearrange("p (t c i) -> p c t i", t=PACK, i=2),
                in1=raw["w", panel, g][:, :, first : first + width].rearrange("p t (c i) -> p c t i", i=2),
                op=mybir.AluOpType.mult,
            )

        def quantize_w(c, g):
            quantize(("w", c, g), "w%d" % WIDTHS[c], 2 * F_PASSES if WIDTHS[c] == BANK else NARROW_W_BUFS)

        def gate(c, g):
            scores(c, g)
            sigmoid(c, g)

        def weigh(c, g):
            sigmoid(c, g)
            multiply(c, g)


        def product(c, m, passes, first=0):
            width = WIDTHS[c]
            for g in passes:
                target = banks["out", c, m][:, first : first + width]
                mx(target, ("h", g), slice(m * P, (m + 1) * P), ("w", c, g), slice(0, width), g == 0, g == F_PASSES - 1)

        def open_product(c, m, passes, role):
            take_bank(role, ("out", c, m))
            product(c, m, passes)

        def store(c, m, copy):
            width = WIDTHS[c]
            result = sb.tile([P, width], F32, name="result", tag="result", bufs=RESULT_BUFS)
            copy(out=result[:], in_=banks["out", c, m][:, 0:width])
            nc.sync.dma_start(out=out[m * P : (m + 1) * P, STARTS[c] : STARTS[c] + width], in_=result[:])

        def store_pair(c, m):
            width = WIDTHS[c]
            result = sb.tile([P, 2 * width], F32, name="result", tag="result", bufs=RESULT_BUFS)
            on_scalar(out=result[:], in_=banks["out", c, m][:])
            rows = out[:, STARTS[c] : STARTS[c] + width].rearrange("(h m p) n -> m p h n", h=2, p=P)
            nc.sync.dma_start(out=rows[m], in_=result[:].rearrange("p (h n) -> p h n", h=2))

        tokens = range(TOKEN_TILES)
        early = range(F_PASSES - 1)
        final = [F_PASSES - 1]

        identity = sb.tile([P, P], F32, name="identity")
        make_identity(nc, identity[:])
        warm = sb.tile([P, 1], F32, name="warm")
        nc.scalar.activation(out=warm[:], in_=identity[:, 0:1], func=ACT.Sigmoid)

        load_a(0)
        load_b(0)
        load_x(0)
        load_x(1)
        load_b(1)
        load_up(0, 1)
        load_w(0, 0)
        load_a(1)
        load_x(2)
        load_x(3)
        load_up(1, 1)
        load_a(2)
        load_w(1, 0)
        load_w(0, 1)
        load_a(3)
        load_up(2, 2)
        load_w(0, 2)
        load_b(2)
        load_w(0, 3)
        for g in range(1, F_PASSES):
            load_w(1, g)
        load_w(2, 0)
        load_w(2, 1)

        turn_a(0, on_scalar)
        interleave_b(0)
        quantize_a(0)
        quantize_b(0)
        turn_x(0)
        turn_x(1)
        gate(0, 0)
        interleave_b(1)
        quantize_x(0)
        quantize_b(1)
        gate(1, 0)
        sort_up(0, 1)
        multiply(0, 0)
        hidden(0, 0)
        turn_a(1, on_vector)
        hidden(0, 1)
        turn_x(2)
        turn_x(3)
        sort_up(1, 1)
        quantize_a(1)
        quantize_w(0, 0)
        quantize_x(1)
        multiply(1, 0)
        load_w(2, 2)
        load_w(2, 3)

        gate(0, 1)
        turn_a(2, on_scalar)
        quantize_w(1, 0)
        quantize_a(2)
        for g, m in ((0, 2), (0, 3), (1, 0), (1, 1)):
            hidden(g, m)
        multiply(0, 1)

        turn_a(3, on_scalar)
        gate(0, 2)
        sort_up(2, 2)
        quantize_a(3)
        quantize_h(0)
        for g, m in ((1, 2), (1, 3), (2, 0), (2, 1)):
            hidden(g, m)
        quantize_w(0, 1)
        multiply(0, 2)

        gate(0, 3)
        quantize_h(1)
        for g, m in ((2, 2), (2, 3), (3, 0), (3, 1)):
            hidden(g, m)
        interleave_b(2)
        quantize_w(0, 2)
        multiply(0, 3)

        gate(1, 1)
        quantize_h(2)
        hidden(3, 2)
        hidden(3, 3)
        quantize_b(2)
        quantize_w(0, 3)
        multiply(1, 1)

        gate(1, 2)
        quantize_h(3)
        for m in tokens:
            open_product(0, m, [0], "other")
        for m in tokens:
            product(0, m, [1])
        quantize_w(1, 1)
        multiply(1, 2)

        gate(1, 3)
        for m in tokens:
            product(0, m, [2])
        multiply(1, 3)
        quantize_w(1, 2)

        scores(2, 0)
        for m in tokens:
            product(0, m, final)
        scores(2, 1)
        weigh(2, 0)
        quantize_w(1, 3)
        for step in range(2):
            pair = (2 * step, 2 * step + 1)
            for m in pair:
                store(0, m, on_scalar)
            scores(2, step + 2)
            for m in pair:
                open_product(1, m, early, "other")
            weigh(2, step + 1)
            quantize_w(2, step)
        scores(3, 0)
        for m in tokens:
            product(1, m, final)
        weigh(2, 3)
        quantize_w(2, 2)
        scores(3, 1)
        weigh(3, 0)
        quantize_w(2, 3)
        store(1, 0, on_scalar)
        store(1, 1, on_scalar)
        scores(3, 2)
        open_product(2, 0, early, "other")
        open_product(2, 1, early, "other")
        weigh(3, 1)
        quantize_w(3, 0)
        scores(3, 3)
        for m in range(2):
            product(2, m, final)
            banks["out", 2, m + 2] = banks["out", 2, m]
            product(2, m + 2, range(F_PASSES), first=WIDTHS[2])
        weigh(3, 2)
        quantize_w(3, 1)
        quantize_w(3, 2)
        weigh(3, 3)
        store_pair(2, 0)
        store_pair(2, 1)
        store(1, 2, on_scalar)
        store(1, 3, on_scalar)
        for m in tokens:
            open_product(3, m, [0], "z")
        for g in early[1:]:
            for m in tokens:
                product(3, m, [g])
        quantize_w(3, 3)
        for m in tokens:
            product(3, m, final)
            store(3, m, on_scalar if m % 2 == 0 else on_vector)
